import numpy as np
import ml_dtypes


def mxq(x, axis, fmt="e4m3"):
    dtype, down = {"e4m3": (ml_dtypes.float8_e4m3fn, 7), "e5m2": (ml_dtypes.float8_e5m2, 14)}[fmt]
    v = np.moveaxis(np.asarray(x, np.float32).astype(ml_dtypes.bfloat16).astype(np.float64), axis, -1)
    blocks = v.reshape(v.shape[:-1] + (-1, 32))
    amax = np.abs(blocks).max(-1, keepdims=True)
    byte = np.maximum(np.where(amax > 0, np.frexp(amax)[1] - 1 + 127, 0) - down, 1)
    scale = np.exp2(byte - 127.0)
    codes = (blocks / scale).astype(np.float32).astype(dtype).astype(np.float64)
    return np.moveaxis((codes * scale).reshape(v.shape), -1, axis)


WIDE = False


def mx_kscale(k):
    if not WIDE:
        return np.ones(k)
    levels = np.array([10, -10, 5, -5, 0])
    if k % 512:
        return np.exp2(np.random.permutation(np.resize(levels, k // 32))).repeat(32)
    a = np.empty((k // 512, 16))
    for p in range(k // 512):
        a[p, :8] = np.random.permutation(np.resize(levels, 8))
        for g in range(8):
            far = levels[np.abs(levels - a[p, g]) >= 10]
            a[p, g + 8] = far[np.random.randint(len(far))]
    return np.exp2(a.ravel()).repeat(32)


def f64(x):
    return np.asarray(x).astype(np.float64)


def striped(idx):
    return np.tile(idx.reshape(-1, 16).T, (8, 1)).astype(np.uint16)


def unstriped(offs):
    return offs[:16].T.reshape(-1).astype(np.int64)


E2M1 = np.array([0.0, 0.5, 1.0, 1.5, 2.0, 3.0, 4.0, 6.0, -0.0, -0.5, -1.0, -1.5, -2.0, -3.0, -4.0, -6.0])


def pack_weight(w, fmt):
    k, n = w.shape
    w = f64(np.asarray(w, np.float32).astype(ml_dtypes.bfloat16)).reshape(k // 32, 32, n)
    amax = np.abs(w).max(1)
    if fmt == "e4m3":
        byte = np.frexp(amax)[1] - 1 + 127 - 7
    else:
        mant, ex = np.frexp(amax / 6.0)
        byte = np.where(mant > 0.5, ex, ex - 1) + 127
    byte = np.clip(np.where(amax > 0, byte, 1), 1, 254)
    scaled = (w * np.exp2(127.0 - byte)[:, None, :]).reshape(k, n).astype(np.float32)
    by_word = np.ascontiguousarray(scaled.reshape(k // 512, 128, 4, n).transpose(0, 1, 3, 2))
    if fmt == "e4m3":
        words = by_word.astype(ml_dtypes.float8_e4m3fn).view(np.uint8)
    else:
        c = by_word.astype(ml_dtypes.float4_e2m1fn).view(np.uint8) & 0xF
        words = (c[..., 0::2] | (c[..., 1::2] << 4)).reshape(k // 512, 128, 2 * n)
    return np.ascontiguousarray(words), np.ascontiguousarray(byte.astype(np.uint8).reshape(k // 512, 16, n))


def unpack_weight(words, scales, fmt):
    g, _, n = scales.shape
    words = np.ascontiguousarray(words).reshape(g, 128, n, -1)
    if fmt == "e4m3":
        vals = words.view(ml_dtypes.float8_e4m3fn).astype(np.float64)
    else:
        nib = np.empty((g, 128, n, 4), np.uint8)
        nib[..., 0::2] = words & 0xF
        nib[..., 1::2] = words >> 4
        vals = E2M1[nib]
    vals = vals * np.repeat(np.exp2(scales.astype(np.float64) - 127.0), 8, axis=1)[..., None]
    return vals.transpose(0, 1, 3, 2).reshape(g * 512, n)


def pack_table(v):
    words, scales = pack_weight(v, "e4m3")
    return np.concatenate([words.reshape(words.shape[0], -1), scales.reshape(scales.shape[0], -1)], axis=1)


def unpack_table(tab):
    g, t = tab.shape[0], tab.shape[1] // 528
    return unpack_weight(tab[:, :512 * t].reshape(g, 128, t, 4), tab[:, 512 * t:].reshape(g, 16, t), "e4m3")


O, K, M, T, S = 512, 1024, 256, 1024, 512


def setup_inputs():
    n = np.random.standard_normal
    s = mx_kscale(K)[:, None]
    w = n((K, M)) / np.sqrt(K) / s
    p_w4 = pack_weight(w[O:], "e2m1")
    return {
        "tab": pack_table(n((K, T)) * s),
        "w8": (w[:O]).astype(np.float32),
        "w4_words": p_w4[0],
        "w4_scales": p_w4[1],
        "offs": striped(np.random.permutation(T)[:S]),
    }


def reference(tab, w8, w4_words, w4_scales, offs):
    tab_ = unpack_table(tab)[:, unstriped(offs)]
    w8_ = mxq(f64(w8), 0, "e4m3")
    w4_ = unpack_weight(w4_words, w4_scales, "e2m1")
    y = w8_.T @ tab_[:O] + w4_.T @ tab_[O:]
    return y

@@ -1,0 +1,136 @@
+from contextlib import ExitStack
+
+import concourse.mybir as mybir
+
+K_PASS, M, T, S = 512, 256, 1024, 512
+FLOPS = 2 * 2 * K_PASS * M * S
+
+F32 = mybir.dt.float32
+BF16 = mybir.dt.bfloat16
+I32 = mybir.dt.int32
+U32 = mybir.dt.uint32
+U16 = mybir.dt.uint16
+U8 = mybir.dt.uint8
+FP8X4 = mybir.dt.float8_e4m3fn_x4
+FP4X4 = mybir.dt.float4_e2m1fn_x4
+
+P = 128
+PACK = 4
+HALVES = M // P
+N_SLICE = 128
+SLICES = S // N_SLICE
+QUAD_BYTES = 4 * T
+WORD_QUADS = P * T * PACK // QUAD_BYTES
+PASS_QUADS = WORD_QUADS + 4
+HOP = (PASS_QUADS + 1) // 7
+
+
+def tile_list_tabo_none_kernel(tc, tab, w8, w4_words, w4_scales, offs, out):
+    nc = tc.nc
+    with ExitStack() as ctx:
+        keep = ctx.enter_context(tc.tile_pool(name="keep", bufs=1))
+        psum = ctx.enter_context(tc.psum_pool(name="psum", bufs=1))
+
+        offsets = keep.tile([P, S // 16], U16, name="offsets")
+        tab_scales = keep.tile([P, T // 4], I32, name="tab_scales", align_bytes=64)
+        tab_words = [keep.tile([P, T], I32, name=f"tab_words{a}", align_bytes=64) for a in range(2)]
+        w8_raw = keep.tile([P, PACK, M], F32, name="w8_raw", align_bytes=64)
+        w8_grouped = keep.tile([P, M, PACK], BF16, name="w8_grouped", align_bytes=64)
+        w8_codes = keep.tile([P, M], U32, name="w8_codes", align_bytes=64)
+        w8_plane = keep.tile([P, M], U8, name="w8_plane", align_bytes=64)
+        w4_codes = keep.tile([P, 2 * M], U8, name="w4_codes", align_bytes=64)
+        w4_plane = keep.tile([P, M // 4], I32, name="w4_plane", align_bytes=64)
+        got_scales = keep.tile([P, S], U8, name="got_scales", align_bytes=64)
+        got_words = [keep.tile([P, S], U32, name=f"got_words{a}", align_bytes=64) for a in range(2)]
+        warm_in = keep.tile([P, 8], F32, name="warm_in")
+        warm_out = keep.tile([P, 8], F32, name="warm_out")
+
+        nc.vector.memset(tab_scales[96:128, :], 0)
+        nc.vector.memset(w4_plane[:], 0)
+        nc.gpsimd.memset(warm_in[:], 0.0)
+        nc.scalar.copy(warm_out[:], warm_in[:])
+
+        nc.sync.dma_start(offsets[:], offs)
+
+        quads = tab.rearrange("a (g b) -> (a g) b", b=QUAD_BYTES).bitcast(I32)
+
+        def as_rows(ap):
+            return ap.rearrange("u (r c) -> u r c", r=4)
+
+        first1 = PASS_QUADS + WORD_QUADS
+        nc.sync.dma_start(tab_scales[0:4, :], as_rows(quads[first1 : first1 + 1, :]))
+        for q in range(3):
+            lo = WORD_QUADS + q
+            nc.sync.dma_start(tab_scales[32 * q + 4 : 32 * q + 36, :], as_rows(quads[lo : lo + 7 * HOP + 1 : HOP, :]))
+        nc.sync.dma_start(tab_scales[100:104, :], as_rows(quads[WORD_QUADS + 3 : WORD_QUADS + 4, :]))
+
+        def load_words(a):
+            nc.sync.dma_start(tab_words[a][:], quads[a * PASS_QUADS : a * PASS_QUADS + WORD_QUADS, :])
+
+        load_words(1)
+        nc.sync.dma_start(w8_raw[:], w8.rearrange("(p j) m -> p j m", j=PACK))
+        nc.sync.dma_start(w4_codes[:].bitcast(I32), w4_words[0].bitcast(I32))
+        for q in range(4):
+            nc.sync.dma_start(w4_plane[32 * q : 32 * q + 4, :], w4_scales[0, 4 * q : 4 * q + 4, :].bitcast(I32))
+        load_words(0)
+
+        nc.vector.tensor_copy(got_scales[:], tab_scales[:].bitcast(U8).indirect(offsets[:]))
+        nc.vector.tensor_copy(got_words[1][:], tab_words[1][:].bitcast(U32).indirect(offsets[:]))
+
+        banks = [[psum.tile([P, N_SLICE], F32, name=f"bank{s}_{h}") for h in range(HALVES)] for s in range(SLICES)]
+        w4_bytes = w4_plane[:].bitcast(U8)
+        for s in range(SLICES):
+            cols = slice(s * N_SLICE, (s + 1) * N_SLICE)
+            for h in range(HALVES):
+                nc.tensor.matmul_mx(
+                    out=banks[s][h][:],
+                    lhsT=w4_codes[:, 2 * P * h : 2 * P * (h + 1)].bitcast(FP4X4),
+                    lhsT_scale=w4_bytes[:, P * h : P * (h + 1)],
+                    rhs=got_words[1][:, cols].bitcast(FP8X4),
+                    rhs_scale=got_scales[:, cols],
+                    start=True,
+                    stop=False,
+                )
+
+        for h, copy in enumerate((nc.vector.tensor_copy, nc.scalar.copy)):
+            ch = slice(P * h, P * (h + 1))
+            copy(
+                w8_grouped[:, ch, :].rearrange("p (c i) t -> p c t i", i=4),
+                w8_raw[:, :, ch].rearrange("p t (c i) -> p c t i", i=4),
+            )
+        for h in range(HALVES):
+            ch = slice(P * h, P * (h + 1))
+            nc.vector.quantize_mx(
+                out=w8_codes[:, ch].bitcast(FP8X4),
+                scales=w8_plane[:, ch],
+                in_=w8_grouped[:, ch, :].rearrange("p m t -> p (m t)"),
+            )
+
+        out_rows = out.rearrange("(h p) j -> p h j", p=P)
+        for s in range(SLICES):
+            cols = slice(s * N_SLICE, (s + 1) * N_SLICE)
+            k16 = N_SLICE // 16
+            nc.vector.tensor_copy(
+                got_words[0][:, cols],
+                tab_words[0][:].bitcast(U32).indirect(offsets[:, s * k16 : (s + 1) * k16]),
+            )
+        for s in range(SLICES):
+            cols = slice(s * N_SLICE, (s + 1) * N_SLICE)
+            result = keep.tile([P, HALVES, N_SLICE], F32, name=f"result{s}")
+            for h in range(HALVES):
+                ch = slice(P * h, P * (h + 1))
+                nc.tensor.matmul_mx(
+                    out=banks[s][h][:],
+                    lhsT=w8_codes[:, ch].bitcast(FP8X4),
+                    lhsT_scale=w8_plane[:, ch],
+                    rhs=got_words[0][:, cols].bitcast(FP8X4),
+                    rhs_scale=got_scales[4:128, cols],
+                    start=False,
+                    stop=True,
+                )
+            for h in range(HALVES):
+                if s == SLICES - 1 and h == 1:
+                    nc.vector.tensor_copy(result[:, h, :], banks[s][h][:])
+                else:
+                    nc.scalar.copy(result[:, h, :], banks[s][h][:])
+            nc.sync.dma_start(out_rows[:, :, cols], result[:])

@@ -48,7 +48,6 @@ def tile_list_tabo_none_kernel(tc, tab, w8, w4_words, w4_scales, offs, out):
         nc.vector.memset(tab_scales[96:128, :], 0)
         nc.vector.memset(w4_plane[:], 0)
         nc.gpsimd.memset(warm_in[:], 0.0)
-        nc.scalar.copy(warm_out[:], warm_in[:])
 
         nc.sync.dma_start(offsets[:], offs)
 
@@ -61,12 +60,14 @@ def tile_list_tabo_none_kernel(tc, tab, w8, w4_words, w4_scales, offs, out):
         nc.sync.dma_start(tab_scales[0:4, :], as_rows(quads[first1 : first1 + 1, :]))
         for q in range(3):
             lo = WORD_QUADS + q
-            nc.sync.dma_start(tab_scales[32 * q + 4 : 32 * q + 36, :], as_rows(quads[lo : lo + 7 * HOP + 1 : HOP, :]))
+            queue = nc.scalar if q < 2 else nc.sync
+            queue.dma_start(tab_scales[32 * q + 4 : 32 * q + 36, :], as_rows(quads[lo : lo + 7 * HOP + 1 : HOP, :]))
         nc.sync.dma_start(tab_scales[100:104, :], as_rows(quads[WORD_QUADS + 3 : WORD_QUADS + 4, :]))
 
         def load_words(a):
             nc.sync.dma_start(tab_words[a][:], quads[a * PASS_QUADS : a * PASS_QUADS + WORD_QUADS, :])
 
+        nc.scalar.copy(warm_out[:], warm_in[:])
         load_words(1)
         nc.sync.dma_start(w8_raw[:], w8.rearrange("(p j) m -> p j m", j=PACK))
         nc.sync.dma_start(w4_codes[:].bitcast(I32), w4_words[0].bitcast(I32))

@@ -16,13 +16,14 @@ FP4X4 = mybir.dt.float4_e2m1fn_x4
 
 P = 128
 PACK = 4
+QUADS = 4
+QUAD = P // QUADS
+ROWS = 4
 HALVES = M // P
 N_SLICE = 128
 SLICES = S // N_SLICE
-QUAD_BYTES = 4 * T
-WORD_QUADS = P * T * PACK // QUAD_BYTES
-PASS_QUADS = WORD_QUADS + 4
-HOP = (PASS_QUADS + 1) // 7
+WORD_BYTES = P * T * PACK
+SPAN = (QUADS - 1) * QUAD + ROWS
 
 
 def tile_list_tabo_none_kernel(tc, tab, w8, w4_words, w4_scales, offs, out):
@@ -41,83 +42,58 @@ def tile_list_tabo_none_kernel(tc, tab, w8, w4_words, w4_scales, offs, out):
         w4_codes = keep.tile([P, 2 * M], U8, name="w4_codes", align_bytes=64)
         w4_plane = keep.tile([P, M // 4], I32, name="w4_plane", align_bytes=64)
         got_scales = keep.tile([P, S], U8, name="got_scales", align_bytes=64)
+        plane1 = keep.tile([P, S // 4], I32, name="plane1", align_bytes=64)
         got_words = [keep.tile([P, S], U32, name=f"got_words{a}", align_bytes=64) for a in range(2)]
         warm_in = keep.tile([P, 8], F32, name="warm_in")
         warm_out = keep.tile([P, 8], F32, name="warm_out")
 
-        nc.vector.memset(tab_scales[96:128, :], 0)
-        nc.vector.memset(w4_plane[:], 0)
-        nc.gpsimd.memset(warm_in[:], 0.0)
+        nc.vector.memset(tab_scales[:], 0)
+        nc.gpsimd.memset(w4_plane[:], 0)
 
         nc.sync.dma_start(offsets[:], offs)
-
-        quads = tab.rearrange("a (g b) -> (a g) b", b=QUAD_BYTES).bitcast(I32)
-
-        def as_rows(ap):
-            return ap.rearrange("u (r c) -> u r c", r=4)
-
-        first1 = PASS_QUADS + WORD_QUADS
-        nc.sync.dma_start(tab_scales[0:4, :], as_rows(quads[first1 : first1 + 1, :]))
-        for q in range(3):
-            lo = WORD_QUADS + q
-            queue = nc.scalar if q < 2 else nc.sync
-            queue.dma_start(tab_scales[32 * q + 4 : 32 * q + 36, :], as_rows(quads[lo : lo + 7 * HOP + 1 : HOP, :]))
-        nc.sync.dma_start(tab_scales[100:104, :], as_rows(quads[WORD_QUADS + 3 : WORD_QUADS + 4, :]))
-
-        def load_words(a):
-            nc.sync.dma_start(tab_words[a][:], quads[a * PASS_QUADS : a * PASS_QUADS + WORD_QUADS, :])
-
-        nc.scalar.copy(warm_out[:], warm_in[:])
-        load_words(1)
         nc.sync.dma_start(w8_raw[:], w8.rearrange("(p j) m -> p j m", j=PACK))
+
+        scale_rows = tab[:, WORD_BYTES:].bitcast(I32).rearrange("a (q r c) -> q a r c", q=QUADS, r=ROWS)
+        for q in range(QUADS):
+            nc.scalar.dma_start(tab_scales[QUAD * q : QUAD * q + 2 * ROWS, :], scale_rows[q])
+        for q in range(QUADS):
+            nc.gpsimd.dma_start(
+                w4_plane[QUAD * q : QUAD * q + ROWS, :], w4_scales[0, ROWS * q : ROWS * (q + 1), :].bitcast(I32)
+            )
+        for a in range(2):
+            nc.sync.dma_start(tab_words[a][:], tab[a, :WORD_BYTES].bitcast(I32).rearrange("(p t) -> p t", p=P))
         nc.sync.dma_start(w4_codes[:].bitcast(I32), w4_words[0].bitcast(I32))
-        for q in range(4):
-            nc.sync.dma_start(w4_plane[32 * q : 32 * q + 4, :], w4_scales[0, 4 * q : 4 * q + 4, :].bitcast(I32))
-        load_words(0)
+
+        nc.vector.memset(warm_in[:], 0.0)
+        nc.vector.memset(plane1[P - QUAD :, :], 0)
+        nc.scalar.copy(warm_out[:], warm_in[:])
 
         nc.vector.tensor_copy(got_scales[:], tab_scales[:].bitcast(U8).indirect(offsets[:]))
-        nc.vector.tensor_copy(got_words[1][:], tab_words[1][:].bitcast(U32).indirect(offsets[:]))
+        nc.sync.dma_start(plane1[:SPAN, :], got_scales[ROWS : ROWS + SPAN, :].bitcast(I32))
 
-        banks = [[psum.tile([P, N_SLICE], F32, name=f"bank{s}_{h}") for h in range(HALVES)] for s in range(SLICES)]
-        w4_bytes = w4_plane[:].bitcast(U8)
-        for s in range(SLICES):
-            cols = slice(s * N_SLICE, (s + 1) * N_SLICE)
-            for h in range(HALVES):
-                nc.tensor.matmul_mx(
-                    out=banks[s][h][:],
-                    lhsT=w4_codes[:, 2 * P * h : 2 * P * (h + 1)].bitcast(FP4X4),
-                    lhsT_scale=w4_bytes[:, P * h : P * (h + 1)],
-                    rhs=got_words[1][:, cols].bitcast(FP8X4),
-                    rhs_scale=got_scales[:, cols],
-                    start=True,
-                    stop=False,
-                )
+        def gather_words(a, s):
+            k16 = N_SLICE // 16
+            nc.vector.tensor_copy(
+                got_words[a][:, s * N_SLICE : (s + 1) * N_SLICE],
+                tab_words[a][:].bitcast(U32).indirect(offsets[:, s * k16 : (s + 1) * k16]),
+            )
 
-        for h, copy in enumerate((nc.vector.tensor_copy, nc.scalar.copy)):
+        for h in range(HALVES):
             ch = slice(P * h, P * (h + 1))
-            copy(
+            nc.scalar.copy(
                 w8_grouped[:, ch, :].rearrange("p (c i) t -> p c t i", i=4),
                 w8_raw[:, :, ch].rearrange("p t (c i) -> p c t i", i=4),
             )
-        for h in range(HALVES):
-            ch = slice(P * h, P * (h + 1))
             nc.vector.quantize_mx(
                 out=w8_codes[:, ch].bitcast(FP8X4),
                 scales=w8_plane[:, ch],
                 in_=w8_grouped[:, ch, :].rearrange("p m t -> p (m t)"),
             )
 
-        out_rows = out.rearrange("(h p) j -> p h j", p=P)
+        banks = [[psum.tile([P, N_SLICE], F32, name=f"bank{s}_{h}") for h in range(HALVES)] for s in range(SLICES)]
         for s in range(SLICES):
             cols = slice(s * N_SLICE, (s + 1) * N_SLICE)
-            k16 = N_SLICE // 16
-            nc.vector.tensor_copy(
-                got_words[0][:, cols],
-                tab_words[0][:].bitcast(U32).indirect(offsets[:, s * k16 : (s + 1) * k16]),
-            )
-        for s in range(SLICES):
-            cols = slice(s * N_SLICE, (s + 1) * N_SLICE)
-            result = keep.tile([P, HALVES, N_SLICE], F32, name=f"result{s}")
+            gather_words(0, s)
             for h in range(HALVES):
                 ch = slice(P * h, P * (h + 1))
                 nc.tensor.matmul_mx(
@@ -125,7 +101,26 @@ def tile_list_tabo_none_kernel(tc, tab, w8, w4_words, w4_scales, offs, out):
                     lhsT=w8_codes[:, ch].bitcast(FP8X4),
                     lhsT_scale=w8_plane[:, ch],
                     rhs=got_words[0][:, cols].bitcast(FP8X4),
-                    rhs_scale=got_scales[4:128, cols],
+                    rhs_scale=got_scales[:, cols],
+                    start=True,
+                    stop=False,
+                )
+
+        out_rows = out.rearrange("(h p) j -> p h j", p=P)
+        w4_bytes = w4_plane[:].bitcast(U8)
+        plane1_bytes = plane1[:].bitcast(U8)
+        for s in range(SLICES):
+            gather_words(1, s)
+        for s in range(SLICES):
+            cols = slice(s * N_SLICE, (s + 1) * N_SLICE)
+            result = keep.tile([P, HALVES, N_SLICE], F32, name=f"result{s}")
+            for h in range(HALVES):
+                nc.tensor.matmul_mx(
+                    out=banks[s][h][:],
+                    lhsT=w4_codes[:, 2 * P * h : 2 * P * (h + 1)].bitcast(FP4X4),
+                    lhsT_scale=w4_bytes[:, P * h : P * (h + 1)],
+                    rhs=got_words[1][:, cols].bitcast(FP8X4),
+                    rhs_scale=plane1_bytes[:, cols],
                     start=False,
                     stop=True,
                 )

@@ -22,8 +22,9 @@ ROWS = 4
 HALVES = M // P
 N_SLICE = 128
 SLICES = S // N_SLICE
-WORD_BYTES = P * T * PACK
-SPAN = (QUADS - 1) * QUAD + ROWS
+WORD_LINES = P * T * PACK // (ROWS * T)
+PASS_LINES = WORD_LINES + QUADS
+SHIFT = QUAD - ROWS
 
 
 def tile_list_tabo_none_kernel(tc, tab, w8, w4_words, w4_scales, offs, out):
@@ -42,58 +43,94 @@ def tile_list_tabo_none_kernel(tc, tab, w8, w4_words, w4_scales, offs, out):
         w4_codes = keep.tile([P, 2 * M], U8, name="w4_codes", align_bytes=64)
         w4_plane = keep.tile([P, M // 4], I32, name="w4_plane", align_bytes=64)
         got_scales = keep.tile([P, S], U8, name="got_scales", align_bytes=64)
-        plane1 = keep.tile([P, S // 4], I32, name="plane1", align_bytes=64)
+        plane0 = keep.tile([P, S // 4], I32, name="plane0", align_bytes=64)
         got_words = [keep.tile([P, S], U32, name=f"got_words{a}", align_bytes=64) for a in range(2)]
         warm_in = keep.tile([P, 8], F32, name="warm_in")
         warm_out = keep.tile([P, 8], F32, name="warm_out")
 
         nc.vector.memset(tab_scales[:], 0)
-        nc.gpsimd.memset(w4_plane[:], 0)
-
         nc.sync.dma_start(offsets[:], offs)
-        nc.sync.dma_start(w8_raw[:], w8.rearrange("(p j) m -> p j m", j=PACK))
+        nc.scalar.dma_start(w4_codes[:].bitcast(I32), w4_words[0].bitcast(I32))
 
-        scale_rows = tab[:, WORD_BYTES:].bitcast(I32).rearrange("a (q r c) -> q a r c", q=QUADS, r=ROWS)
-        for q in range(QUADS):
-            nc.scalar.dma_start(tab_scales[QUAD * q : QUAD * q + 2 * ROWS, :], scale_rows[q])
-        for q in range(QUADS):
-            nc.gpsimd.dma_start(
+        lines = tab.rearrange("a (g b) -> (a g) b", b=ROWS * T).bitcast(I32)
+
+        def scale_lines(first, count):
+            picked = lines[first : first + (count - 1) * (PASS_LINES + 1) + 1 : PASS_LINES + 1, :]
+            return picked.rearrange("u (r c) -> u r c", r=ROWS)
+
+        for q in range(1, QUADS):
+            queue = nc.sync if q == 1 else nc.scalar
+            queue.dma_start(tab_scales[QUAD * q - ROWS : QUAD * q + ROWS, :], scale_lines(WORD_LINES + q - 1, 2))
+        nc.sync.dma_start(tab_scales[:ROWS, :], scale_lines(PASS_LINES + WORD_LINES, 1))
+        nc.sync.dma_start(tab_scales[P - ROWS :, :], scale_lines(WORD_LINES + QUADS - 1, 1))
+
+        def load_words(a):
+            nc.sync.dma_start(tab_words[a][:], lines[a * PASS_LINES : a * PASS_LINES + WORD_LINES, :])
+
+        def load_w4_scales(q):
+            nc.sync.dma_start(
                 w4_plane[QUAD * q : QUAD * q + ROWS, :], w4_scales[0, ROWS * q : ROWS * (q + 1), :].bitcast(I32)
             )
-        for a in range(2):
-            nc.sync.dma_start(tab_words[a][:], tab[a, :WORD_BYTES].bitcast(I32).rearrange("(p t) -> p t", p=P))
-        nc.sync.dma_start(w4_codes[:].bitcast(I32), w4_words[0].bitcast(I32))
 
+        load_words(1)
         nc.vector.memset(warm_in[:], 0.0)
-        nc.vector.memset(plane1[P - QUAD :, :], 0)
+        nc.vector.memset(w4_plane[:], 0)
+        load_w4_scales(0)
+        nc.sync.dma_start(w8_raw[:], w8.rearrange("(p j) m -> p j m", j=PACK))
+        for q in range(1, QUADS):
+            load_w4_scales(q)
+        load_words(0)
+        nc.vector.memset(plane0[P // 2 :, :], 0)
         nc.scalar.copy(warm_out[:], warm_in[:])
 
         nc.vector.tensor_copy(got_scales[:], tab_scales[:].bitcast(U8).indirect(offsets[:]))
-        nc.sync.dma_start(plane1[:SPAN, :], got_scales[ROWS : ROWS + SPAN, :].bitcast(I32))
-
-        def gather_words(a, s):
-            k16 = N_SLICE // 16
-            nc.vector.tensor_copy(
-                got_words[a][:, s * N_SLICE : (s + 1) * N_SLICE],
-                tab_words[a][:].bitcast(U32).indirect(offsets[:, s * k16 : (s + 1) * k16]),
+        for first, count in ((0, P // 2), (2 * QUAD, ROWS), (3 * QUAD, ROWS)):
+            nc.sync.dma_start(
+                plane0[first : first + count, :], got_scales[SHIFT + first : SHIFT + first + count, :].bitcast(I32)
             )
 
-        for h in range(HALVES):
+        def gather_words(a, lo, hi):
+            nc.vector.tensor_copy(
+                got_words[a][:, lo:hi],
+                tab_words[a][:].bitcast(U32).indirect(offsets[:, lo // 16 : hi // 16]),
+            )
+
+        banks = [[psum.tile([P, N_SLICE], F32, name=f"bank{s}_{h}") for h in range(HALVES)] for s in range(SLICES)]
+        w4_bytes = w4_plane[:].bitcast(U8)
+        gather_words(1, 0, S)
+        for s in range(SLICES):
+            cols = slice(s * N_SLICE, (s + 1) * N_SLICE)
+            for h in range(HALVES):
+                nc.tensor.matmul_mx(
+                    out=banks[s][h][:],
+                    lhsT=w4_codes[:, 2 * P * h : 2 * P * (h + 1)].bitcast(FP4X4),
+                    lhsT_scale=w4_bytes[:, P * h : P * (h + 1)],
+                    rhs=got_words[1][:, cols].bitcast(FP8X4),
+                    rhs_scale=got_scales[:, cols],
+                    start=True,
+                    stop=False,
+                )
+
+        for h, copy in enumerate((nc.vector.tensor_copy, nc.scalar.copy)):
             ch = slice(P * h, P * (h + 1))
-            nc.scalar.copy(
+            copy(
                 w8_grouped[:, ch, :].rearrange("p (c i) t -> p c t i", i=4),
                 w8_raw[:, :, ch].rearrange("p t (c i) -> p c t i", i=4),
             )
+        for h in reversed(range(HALVES)):
+            ch = slice(P * h, P * (h + 1))
             nc.vector.quantize_mx(
                 out=w8_codes[:, ch].bitcast(FP8X4),
                 scales=w8_plane[:, ch],
                 in_=w8_grouped[:, ch, :].rearrange("p m t -> p (m t)"),
             )
 
-        banks = [[psum.tile([P, N_SLICE], F32, name=f"bank{s}_{h}") for h in range(HALVES)] for s in range(SLICES)]
+        plane0_bytes = plane0[:].bitcast(U8)
+        for s in range(SLICES):
+            gather_words(0, s * N_SLICE, (s + 1) * N_SLICE)
+        results = [keep.tile([P, S], F32, name=f"result{h}") for h in range(HALVES)]
         for s in range(SLICES):
             cols = slice(s * N_SLICE, (s + 1) * N_SLICE)
-            gather_words(0, s)
             for h in range(HALVES):
                 ch = slice(P * h, P * (h + 1))
                 nc.tensor.matmul_mx(
@@ -101,32 +138,13 @@ def tile_list_tabo_none_kernel(tc, tab, w8, w4_words, w4_scales, offs, out):
                     lhsT=w8_codes[:, ch].bitcast(FP8X4),
                     lhsT_scale=w8_plane[:, ch],
                     rhs=got_words[0][:, cols].bitcast(FP8X4),
-                    rhs_scale=got_scales[:, cols],
-                    start=True,
-                    stop=False,
-                )
-
-        out_rows = out.rearrange("(h p) j -> p h j", p=P)
-        w4_bytes = w4_plane[:].bitcast(U8)
-        plane1_bytes = plane1[:].bitcast(U8)
-        for s in range(SLICES):
-            gather_words(1, s)
-        for s in range(SLICES):
-            cols = slice(s * N_SLICE, (s + 1) * N_SLICE)
-            result = keep.tile([P, HALVES, N_SLICE], F32, name=f"result{s}")
-            for h in range(HALVES):
-                nc.tensor.matmul_mx(
-                    out=banks[s][h][:],
-                    lhsT=w4_codes[:, 2 * P * h : 2 * P * (h + 1)].bitcast(FP4X4),
-                    lhsT_scale=w4_bytes[:, P * h : P * (h + 1)],
-                    rhs=got_words[1][:, cols].bitcast(FP8X4),
-                    rhs_scale=plane1_bytes[:, cols],
+                    rhs_scale=plane0_bytes[:, cols],
                     start=False,
                     stop=True,
                 )
             for h in range(HALVES):
-                if s == SLICES - 1 and h == 1:
-                    nc.vector.tensor_copy(result[:, h, :], banks[s][h][:])
-                else:
-                    nc.scalar.copy(result[:, h, :], banks[s][h][:])
-            nc.sync.dma_start(out_rows[:, :, cols], result[:])
+                copy = nc.vector.tensor_copy if s == SLICES - 1 and h == 1 else nc.scalar.copy
+                copy(results[h][:, cols], banks[s][h][:])
+                if s % 2:
+                    pair = slice((s - 1) * N_SLICE, (s + 1) * N_SLICE)
+                    nc.sync.dma_start(out[P * h : P * (h + 1), pair], results[h][:, pair])

@@ -24,7 +24,7 @@ N_SLICE = 128
 SLICES = S // N_SLICE
 WORD_LINES = P * T * PACK // (ROWS * T)
 PASS_LINES = WORD_LINES + QUADS
-SHIFT = QUAD - ROWS
+SPAN = (QUADS - 1) * QUAD + ROWS
 
 
 def tile_list_tabo_none_kernel(tc, tab, w8, w4_words, w4_scales, offs, out):
@@ -50,7 +50,7 @@ def tile_list_tabo_none_kernel(tc, tab, w8, w4_words, w4_scales, offs, out):
 
         nc.vector.memset(tab_scales[:], 0)
         nc.sync.dma_start(offsets[:], offs)
-        nc.scalar.dma_start(w4_codes[:].bitcast(I32), w4_words[0].bitcast(I32))
+        nc.sync.dma_start(w4_codes[:].bitcast(I32), w4_words[0].bitcast(I32))
 
         lines = tab.rearrange("a (g b) -> (a g) b", b=ROWS * T).bitcast(I32)
 
@@ -67,27 +67,20 @@ def tile_list_tabo_none_kernel(tc, tab, w8, w4_words, w4_scales, offs, out):
         def load_words(a):
             nc.sync.dma_start(tab_words[a][:], lines[a * PASS_LINES : a * PASS_LINES + WORD_LINES, :])
 
-        def load_w4_scales(q):
+        load_words(1)
+        nc.sync.dma_start(w8_raw[:], w8.rearrange("(p j) m -> p j m", j=PACK))
+        nc.vector.memset(warm_in[:], 0.0)
+        nc.vector.memset(w4_plane[:], 0)
+        for q in range(QUADS):
             nc.sync.dma_start(
                 w4_plane[QUAD * q : QUAD * q + ROWS, :], w4_scales[0, ROWS * q : ROWS * (q + 1), :].bitcast(I32)
             )
-
-        load_words(1)
-        nc.vector.memset(warm_in[:], 0.0)
-        nc.vector.memset(w4_plane[:], 0)
-        load_w4_scales(0)
-        nc.sync.dma_start(w8_raw[:], w8.rearrange("(p j) m -> p j m", j=PACK))
-        for q in range(1, QUADS):
-            load_w4_scales(q)
         load_words(0)
-        nc.vector.memset(plane0[P // 2 :, :], 0)
+        nc.vector.memset(plane0[P - QUAD :, :], 0)
         nc.scalar.copy(warm_out[:], warm_in[:])
 
         nc.vector.tensor_copy(got_scales[:], tab_scales[:].bitcast(U8).indirect(offsets[:]))
-        for first, count in ((0, P // 2), (2 * QUAD, ROWS), (3 * QUAD, ROWS)):
-            nc.sync.dma_start(
-                plane0[first : first + count, :], got_scales[SHIFT + first : SHIFT + first + count, :].bitcast(I32)
-            )
+        nc.sync.dma_start(plane0[:SPAN, :], got_scales[P - SPAN :, :].bitcast(I32))
 
         def gather_words(a, lo, hi):
             nc.vector.tensor_copy(

@@ -45,8 +45,6 @@ def tile_list_tabo_none_kernel(tc, tab, w8, w4_words, w4_scales, offs, out):
         got_scales = keep.tile([P, S], U8, name="got_scales", align_bytes=64)
         plane0 = keep.tile([P, S // 4], I32, name="plane0", align_bytes=64)
         got_words = [keep.tile([P, S], U32, name=f"got_words{a}", align_bytes=64) for a in range(2)]
-        warm_in = keep.tile([P, 8], F32, name="warm_in")
-        warm_out = keep.tile([P, 8], F32, name="warm_out")
 
         nc.vector.memset(tab_scales[:], 0)
         nc.sync.dma_start(offsets[:], offs)
@@ -69,7 +67,6 @@ def tile_list_tabo_none_kernel(tc, tab, w8, w4_words, w4_scales, offs, out):
 
         load_words(1)
         nc.sync.dma_start(w8_raw[:], w8.rearrange("(p j) m -> p j m", j=PACK))
-        nc.vector.memset(warm_in[:], 0.0)
         nc.vector.memset(w4_plane[:], 0)
         for q in range(QUADS):
             nc.sync.dma_start(
@@ -77,7 +74,6 @@ def tile_list_tabo_none_kernel(tc, tab, w8, w4_words, w4_scales, offs, out):
             )
         load_words(0)
         nc.vector.memset(plane0[P - QUAD :, :], 0)
-        nc.scalar.copy(warm_out[:], warm_in[:])
 
         nc.vector.tensor_copy(got_scales[:], tab_scales[:].bitcast(U8).indirect(offsets[:]))
         nc.sync.dma_start(plane0[:SPAN, :], got_scales[P - SPAN :, :].bitcast(I32))

@@ -24,7 +24,7 @@ N_SLICE = 128
 SLICES = S // N_SLICE
 WORD_LINES = P * T * PACK // (ROWS * T)
 PASS_LINES = WORD_LINES + QUADS
-SPAN = (QUADS - 1) * QUAD + ROWS
+PARKED = P - QUADS * ROWS
 
 
 def tile_list_tabo_none_kernel(tc, tab, w8, w4_words, w4_scales, offs, out):
@@ -46,21 +46,17 @@ def tile_list_tabo_none_kernel(tc, tab, w8, w4_words, w4_scales, offs, out):
         plane0 = keep.tile([P, S // 4], I32, name="plane0", align_bytes=64)
         got_words = [keep.tile([P, S], U32, name=f"got_words{a}", align_bytes=64) for a in range(2)]
 
-        nc.vector.memset(tab_scales[:], 0)
+        scale_rows = tab[:, P * T * PACK :].rearrange("a (r t) -> a r t", t=T).bitcast(I32)
+        nc.vector.memset(tab_scales[:PARKED, :], 0)
         nc.sync.dma_start(offsets[:], offs)
+        nc.scalar.dma_start(tab_scales[PARKED:, :], scale_rows[0])
         nc.sync.dma_start(w4_codes[:].bitcast(I32), w4_words[0].bitcast(I32))
 
         lines = tab.rearrange("a (g b) -> (a g) b", b=ROWS * T).bitcast(I32)
 
-        def scale_lines(first, count):
-            picked = lines[first : first + (count - 1) * (PASS_LINES + 1) + 1 : PASS_LINES + 1, :]
-            return picked.rearrange("u (r c) -> u r c", r=ROWS)
-
-        for q in range(1, QUADS):
-            queue = nc.sync if q == 1 else nc.scalar
-            queue.dma_start(tab_scales[QUAD * q - ROWS : QUAD * q + ROWS, :], scale_lines(WORD_LINES + q - 1, 2))
-        nc.sync.dma_start(tab_scales[:ROWS, :], scale_lines(PASS_LINES + WORD_LINES, 1))
-        nc.sync.dma_start(tab_scales[P - ROWS :, :], scale_lines(WORD_LINES + QUADS - 1, 1))
+        for q in range(QUADS):
+            queue = nc.scalar if q % 2 else nc.sync
+            queue.dma_start(tab_scales[QUAD * q : QUAD * q + ROWS, :], scale_rows[1, ROWS * q : ROWS * (q + 1)])
 
         def load_words(a):
             nc.sync.dma_start(tab_words[a][:], lines[a * PASS_LINES : a * PASS_LINES + WORD_LINES, :])
@@ -73,10 +69,14 @@ def tile_list_tabo_none_kernel(tc, tab, w8, w4_words, w4_scales, offs, out):
                 w4_plane[QUAD * q : QUAD * q + ROWS, :], w4_scales[0, ROWS * q : ROWS * (q + 1), :].bitcast(I32)
             )
         load_words(0)
-        nc.vector.memset(plane0[P - QUAD :, :], 0)
+        nc.vector.memset(plane0[:], 0)
 
         nc.vector.tensor_copy(got_scales[:], tab_scales[:].bitcast(U8).indirect(offsets[:]))
-        nc.sync.dma_start(plane0[:SPAN, :], got_scales[P - SPAN :, :].bitcast(I32))
+        for q in range(QUADS):
+            nc.sync.dma_start(
+                plane0[QUAD * q : QUAD * q + ROWS, :],
+                got_scales[PARKED + ROWS * q : PARKED + ROWS * (q + 1), :].bitcast(I32),
+            )
 
         def gather_words(a, lo, hi):
             nc.vector.tensor_copy(

@@ -55,19 +55,20 @@ def tile_list_tabo_none_kernel(tc, tab, w8, w4_words, w4_scales, offs, out):
         lines = tab.rearrange("a (g b) -> (a g) b", b=ROWS * T).bitcast(I32)
 
         for q in range(QUADS):
-            queue = nc.scalar if q % 2 else nc.sync
+            queue = nc.scalar if q == 1 else nc.sync
             queue.dma_start(tab_scales[QUAD * q : QUAD * q + ROWS, :], scale_rows[1, ROWS * q : ROWS * (q + 1)])
 
         def load_words(a):
             nc.sync.dma_start(tab_words[a][:], lines[a * PASS_LINES : a * PASS_LINES + WORD_LINES, :])
 
         load_words(1)
-        nc.sync.dma_start(w8_raw[:], w8.rearrange("(p j) m -> p j m", j=PACK))
         nc.vector.memset(w4_plane[:], 0)
         for q in range(QUADS):
             nc.sync.dma_start(
                 w4_plane[QUAD * q : QUAD * q + ROWS, :], w4_scales[0, ROWS * q : ROWS * (q + 1), :].bitcast(I32)
             )
+            if q == 0:
+                nc.sync.dma_start(w8_raw[:], w8.rearrange("(p j) m -> p j m", j=PACK))
         load_words(0)
         nc.vector.memset(plane0[:], 0)
 

@@ -24,6 +24,7 @@ N_SLICE = 128
 SLICES = S // N_SLICE
 WORD_LINES = P * T * PACK // (ROWS * T)
 PASS_LINES = WORD_LINES + QUADS
+EARLY = 2
 PARKED = P - QUADS * ROWS
 
 
@@ -50,7 +51,9 @@ def tile_list_tabo_none_kernel(tc, tab, w8, w4_words, w4_scales, offs, out):
         nc.vector.memset(tab_scales[:PARKED, :], 0)
         nc.sync.dma_start(offsets[:], offs)
         nc.scalar.dma_start(tab_scales[PARKED:, :], scale_rows[0])
-        nc.sync.dma_start(w4_codes[:].bitcast(I32), w4_words[0].bitcast(I32))
+        nc.gpsimd.dma_start(w4_codes[:].bitcast(I32), w4_words[0].bitcast(I32))
+        w8_rows = w8.rearrange("(p j) m -> p j m", j=PACK)
+        nc.sync.dma_start(w8_raw[:, :EARLY, :], w8_rows[:, :EARLY, :])
 
         lines = tab.rearrange("a (g b) -> (a g) b", b=ROWS * T).bitcast(I32)
 
@@ -68,7 +71,7 @@ def tile_list_tabo_none_kernel(tc, tab, w8, w4_words, w4_scales, offs, out):
                 w4_plane[QUAD * q : QUAD * q + ROWS, :], w4_scales[0, ROWS * q : ROWS * (q + 1), :].bitcast(I32)
             )
             if q == 0:
-                nc.sync.dma_start(w8_raw[:], w8.rearrange("(p j) m -> p j m", j=PACK))
+                nc.sync.dma_start(w8_raw[:, EARLY:, :], w8_rows[:, EARLY:, :])
         load_words(0)
         nc.vector.memset(plane0[:], 0)
 

@@ -24,7 +24,7 @@ N_SLICE = 128
 SLICES = S // N_SLICE
 WORD_LINES = P * T * PACK // (ROWS * T)
 PASS_LINES = WORD_LINES + QUADS
-EARLY = 2
+EARLY = 1
 PARKED = P - QUADS * ROWS
 
 
@@ -51,7 +51,6 @@ def tile_list_tabo_none_kernel(tc, tab, w8, w4_words, w4_scales, offs, out):
         nc.vector.memset(tab_scales[:PARKED, :], 0)
         nc.sync.dma_start(offsets[:], offs)
         nc.scalar.dma_start(tab_scales[PARKED:, :], scale_rows[0])
-        nc.gpsimd.dma_start(w4_codes[:].bitcast(I32), w4_words[0].bitcast(I32))
         w8_rows = w8.rearrange("(p j) m -> p j m", j=PACK)
         nc.sync.dma_start(w8_raw[:, :EARLY, :], w8_rows[:, :EARLY, :])
 
@@ -72,6 +71,7 @@ def tile_list_tabo_none_kernel(tc, tab, w8, w4_words, w4_scales, offs, out):
             )
             if q == 0:
                 nc.sync.dma_start(w8_raw[:, EARLY:, :], w8_rows[:, EARLY:, :])
+        nc.sync.dma_start(w4_codes[:].bitcast(I32), w4_words[0].bitcast(I32))
         load_words(0)
         nc.vector.memset(plane0[:], 0)
 

@@ -16,16 +16,19 @@ FP4X4 = mybir.dt.float4_e2m1fn_x4
 
 P = 128
 PACK = 4
+WORD = 4
+GROUP = 16
 QUADS = 4
 QUAD = P // QUADS
 ROWS = 4
+PARKED = P - QUADS * ROWS
 HALVES = M // P
 N_SLICE = 128
 SLICES = S // N_SLICE
-WORD_LINES = P * T * PACK // (ROWS * T)
-PASS_LINES = WORD_LINES + QUADS
-EARLY = 1
-PARKED = P - QUADS * ROWS
+PASS_LINES = P + QUADS
+EARLY = 384
+VECTOR_COLS = 96
+RUN = 4
 
 
 def tile_list_tabo_none_kernel(tc, tab, w8, w4_words, w4_scales, offs, out):
@@ -34,63 +37,65 @@ def tile_list_tabo_none_kernel(tc, tab, w8, w4_words, w4_scales, offs, out):
         keep = ctx.enter_context(tc.tile_pool(name="keep", bufs=1))
         psum = ctx.enter_context(tc.psum_pool(name="psum", bufs=1))
 
-        offsets = keep.tile([P, S // 16], U16, name="offsets")
-        tab_scales = keep.tile([P, T // 4], I32, name="tab_scales", align_bytes=64)
+        offsets = keep.tile([P, S // GROUP], U16, name="offsets")
+        tab_scales = keep.tile([P, T // WORD], I32, name="tab_scales", align_bytes=64)
         tab_words = [keep.tile([P, T], I32, name=f"tab_words{a}", align_bytes=64) for a in range(2)]
         w8_raw = keep.tile([P, PACK, M], F32, name="w8_raw", align_bytes=64)
         w8_grouped = keep.tile([P, M, PACK], BF16, name="w8_grouped", align_bytes=64)
         w8_codes = keep.tile([P, M], U32, name="w8_codes", align_bytes=64)
         w8_plane = keep.tile([P, M], U8, name="w8_plane", align_bytes=64)
         w4_codes = keep.tile([P, 2 * M], U8, name="w4_codes", align_bytes=64)
-        w4_plane = keep.tile([P, M // 4], I32, name="w4_plane", align_bytes=64)
+        w4_plane = keep.tile([P, M // WORD], I32, name="w4_plane", align_bytes=64)
         got_scales = keep.tile([P, S], U8, name="got_scales", align_bytes=64)
-        plane0 = keep.tile([P, S // 4], I32, name="plane0", align_bytes=64)
+        plane0 = keep.tile([P, S // WORD], I32, name="plane0", align_bytes=64)
         got_words = [keep.tile([P, S], U32, name=f"got_words{a}", align_bytes=64) for a in range(2)]
+
+        def quad_rows(tile, q):
+            return tile[QUAD * q : QUAD * q + ROWS, :]
 
         scale_rows = tab[:, P * T * PACK :].rearrange("a (r t) -> a r t", t=T).bitcast(I32)
         nc.vector.memset(tab_scales[:PARKED, :], 0)
         nc.sync.dma_start(offsets[:], offs)
         nc.scalar.dma_start(tab_scales[PARKED:, :], scale_rows[0])
-        w8_rows = w8.rearrange("(p j) m -> p j m", j=PACK)
-        nc.sync.dma_start(w8_raw[:, :EARLY, :], w8_rows[:, :EARLY, :])
 
-        lines = tab.rearrange("a (g b) -> (a g) b", b=ROWS * T).bitcast(I32)
+        w8_rows = w8.rearrange("(p j) m -> p (j m)", j=PACK)
+        w8_flat = w8_raw[:].rearrange("p j m -> p (j m)")
+        nc.sync.dma_start(w8_flat[:, :EARLY], w8_rows[:, :EARLY])
 
         for q in range(QUADS):
             queue = nc.scalar if q == 1 else nc.sync
-            queue.dma_start(tab_scales[QUAD * q : QUAD * q + ROWS, :], scale_rows[1, ROWS * q : ROWS * (q + 1)])
+            queue.dma_start(quad_rows(tab_scales, q), scale_rows[1, ROWS * q : ROWS * (q + 1)])
+
+        lines = tab.rearrange("a (g b) -> (a g) b", b=PACK * T).bitcast(I32)
 
         def load_words(a):
-            nc.sync.dma_start(tab_words[a][:], lines[a * PASS_LINES : a * PASS_LINES + WORD_LINES, :])
+            nc.sync.dma_start(tab_words[a][:], lines[a * PASS_LINES : a * PASS_LINES + P, :])
 
         load_words(1)
         nc.vector.memset(w4_plane[:], 0)
         for q in range(QUADS):
-            nc.sync.dma_start(
-                w4_plane[QUAD * q : QUAD * q + ROWS, :], w4_scales[0, ROWS * q : ROWS * (q + 1), :].bitcast(I32)
-            )
+            nc.sync.dma_start(quad_rows(w4_plane, q), w4_scales[0, ROWS * q : ROWS * (q + 1), :].bitcast(I32))
             if q == 0:
-                nc.sync.dma_start(w8_raw[:, EARLY:, :], w8_rows[:, EARLY:, :])
+                nc.sync.dma_start(w8_flat[:, EARLY:], w8_rows[:, EARLY:])
         nc.sync.dma_start(w4_codes[:].bitcast(I32), w4_words[0].bitcast(I32))
         load_words(0)
         nc.vector.memset(plane0[:], 0)
 
         nc.vector.tensor_copy(got_scales[:], tab_scales[:].bitcast(U8).indirect(offsets[:]))
         for q in range(QUADS):
-            nc.sync.dma_start(
-                plane0[QUAD * q : QUAD * q + ROWS, :],
-                got_scales[PARKED + ROWS * q : PARKED + ROWS * (q + 1), :].bitcast(I32),
-            )
+            parked = got_scales[PARKED + ROWS * q : PARKED + ROWS * (q + 1), :]
+            nc.sync.dma_start(quad_rows(plane0, q), parked.bitcast(I32))
 
         def gather_words(a, lo, hi):
             nc.vector.tensor_copy(
                 got_words[a][:, lo:hi],
-                tab_words[a][:].bitcast(U32).indirect(offsets[:, lo // 16 : hi // 16]),
+                tab_words[a][:].bitcast(U32).indirect(offsets[:, lo // GROUP : hi // GROUP]),
             )
 
         banks = [[psum.tile([P, N_SLICE], F32, name=f"bank{s}_{h}") for h in range(HALVES)] for s in range(SLICES)]
         w4_bytes = w4_plane[:].bitcast(U8)
-        gather_words(1, 0, S)
+        for lo in range(0, S, S // 2):
+            gather_words(1, lo, lo + S // 2)
         for s in range(SLICES):
             cols = slice(s * N_SLICE, (s + 1) * N_SLICE)
             for h in range(HALVES):
@@ -104,11 +109,14 @@ def tile_list_tabo_none_kernel(tc, tab, w8, w4_words, w4_scales, offs, out):
                     stop=False,
                 )
 
-        for h, copy in enumerate((nc.vector.tensor_copy, nc.scalar.copy)):
-            ch = slice(P * h, P * (h + 1))
+        for copy, ch in (
+            (nc.scalar.copy, slice(P, M)),
+            (nc.vector.tensor_copy, slice(0, VECTOR_COLS)),
+            (nc.scalar.copy, slice(VECTOR_COLS, P)),
+        ):
             copy(
-                w8_grouped[:, ch, :].rearrange("p (c i) t -> p c t i", i=4),
-                w8_raw[:, :, ch].rearrange("p t (c i) -> p c t i", i=4),
+                w8_grouped[:, ch, :].rearrange("p (c i) t -> p c t i", i=RUN),
+                w8_raw[:, :, ch].rearrange("p t (c i) -> p c t i", i=RUN),
             )
         for h in reversed(range(HALVES)):
             ch = slice(P * h, P * (h + 1))
@@ -136,7 +144,8 @@ def tile_list_tabo_none_kernel(tc, tab, w8, w4_words, w4_scales, offs, out):
                     stop=True,
                 )
             for h in range(HALVES):
-                copy = nc.vector.tensor_copy if s == SLICES - 1 and h == 1 else nc.scalar.copy
+                is_last_bank = s == SLICES - 1 and h == HALVES - 1
+                copy = nc.vector.tensor_copy if is_last_bank else nc.scalar.copy
                 copy(results[h][:, cols], banks[s][h][:])
                 if s % 2:
                     pair = slice((s - 1) * N_SLICE, (s + 1) * N_SLICE)

@@ -50,8 +50,8 @@ def tile_list_tabo_none_kernel(tc, tab, w8, w4_words, w4_scales, offs, out):
         plane0 = keep.tile([P, S // WORD], I32, name="plane0", align_bytes=64)
         got_words = [keep.tile([P, S], U32, name=f"got_words{a}", align_bytes=64) for a in range(2)]
 
-        def quad_rows(tile, q):
-            return tile[QUAD * q : QUAD * q + ROWS, :]
+        def plane_row(tile, r):
+            return tile[r::QUAD, :]
 
         scale_rows = tab[:, P * T * PACK :].rearrange("a (r t) -> a r t", t=T).bitcast(I32)
         nc.vector.memset(tab_scales[:PARKED, :], 0)
@@ -62,9 +62,9 @@ def tile_list_tabo_none_kernel(tc, tab, w8, w4_words, w4_scales, offs, out):
         w8_flat = w8_raw[:].rearrange("p j m -> p (j m)")
         nc.sync.dma_start(w8_flat[:, :EARLY], w8_rows[:, :EARLY])
 
-        for q in range(QUADS):
-            queue = nc.scalar if q == 1 else nc.sync
-            queue.dma_start(quad_rows(tab_scales, q), scale_rows[1, ROWS * q : ROWS * (q + 1)])
+        for r in range(ROWS):
+            queue = nc.scalar if r == 1 else nc.sync
+            queue.dma_start(plane_row(tab_scales, r), scale_rows[1, r::ROWS])
 
         lines = tab.rearrange("a (g b) -> (a g) b", b=PACK * T).bitcast(I32)
 
@@ -73,18 +73,17 @@ def tile_list_tabo_none_kernel(tc, tab, w8, w4_words, w4_scales, offs, out):
 
         load_words(1)
         nc.vector.memset(w4_plane[:], 0)
-        for q in range(QUADS):
-            nc.sync.dma_start(quad_rows(w4_plane, q), w4_scales[0, ROWS * q : ROWS * (q + 1), :].bitcast(I32))
-            if q == 0:
+        for r in range(ROWS):
+            nc.sync.dma_start(plane_row(w4_plane, r), w4_scales[0].bitcast(I32)[r::ROWS])
+            if r == 0:
                 nc.sync.dma_start(w8_flat[:, EARLY:], w8_rows[:, EARLY:])
         nc.sync.dma_start(w4_codes[:].bitcast(I32), w4_words[0].bitcast(I32))
         load_words(0)
         nc.vector.memset(plane0[:], 0)
 
         nc.vector.tensor_copy(got_scales[:], tab_scales[:].bitcast(U8).indirect(offsets[:]))
-        for q in range(QUADS):
-            parked = got_scales[PARKED + ROWS * q : PARKED + ROWS * (q + 1), :]
-            nc.sync.dma_start(quad_rows(plane0, q), parked.bitcast(I32))
+        for r in range(ROWS):
+            nc.sync.dma_start(plane_row(plane0, r), got_scales[:].bitcast(I32)[PARKED + r :: ROWS, :])
 
         def gather_words(a, lo, hi):
             nc.vector.tensor_copy(

@@ -131,7 +131,8 @@ def tile_list_tabo_none_kernel(tc, tab, w8, w4_words, w4_scales, offs, out):
         results = [keep.tile([P, S], F32, name=f"result{h}") for h in range(HALVES)]
         for s in range(SLICES):
             cols = slice(s * N_SLICE, (s + 1) * N_SLICE)
-            for h in range(HALVES):
+            order = (0, 1) if s == 1 else (1, 0)
+            for h in order:
                 ch = slice(P * h, P * (h + 1))
                 nc.tensor.matmul_mx(
                     out=banks[s][h][:],
@@ -142,10 +143,11 @@ def tile_list_tabo_none_kernel(tc, tab, w8, w4_words, w4_scales, offs, out):
                     start=False,
                     stop=True,
                 )
-            for h in range(HALVES):
-                is_last_bank = s == SLICES - 1 and h == HALVES - 1
+            for h in order:
+                is_last_bank = s == SLICES - 1 and h == order[-1]
                 copy = nc.vector.tensor_copy if is_last_bank else nc.scalar.copy
                 copy(results[h][:, cols], banks[s][h][:])
-                if s % 2:
-                    pair = slice((s - 1) * N_SLICE, (s + 1) * N_SLICE)
-                    nc.sync.dma_start(out[P * h : P * (h + 1), pair], results[h][:, pair])
+                if (s + h) % 2 or s == SLICES - 1:
+                    first = s if h and s in (0, SLICES - 1) else s - 1
+                    span = slice(first * N_SLICE, (s + 1) * N_SLICE)
+                    nc.sync.dma_start(out[P * h : P * (h + 1), span], results[h][:, span])

@@ -28,6 +28,7 @@ SLICES = S // N_SLICE
 PASS_LINES = P + QUADS
 EARLY = 384
 VECTOR_COLS = 96
+LINE = 256
 RUN = 4
 
 
@@ -38,17 +39,17 @@ def tile_list_tabo_none_kernel(tc, tab, w8, w4_words, w4_scales, offs, out):
         psum = ctx.enter_context(tc.psum_pool(name="psum", bufs=1))
 
         offsets = keep.tile([P, S // GROUP], U16, name="offsets")
-        tab_scales = keep.tile([P, T // WORD], I32, name="tab_scales", align_bytes=64)
-        tab_words = [keep.tile([P, T], I32, name=f"tab_words{a}", align_bytes=64) for a in range(2)]
-        w8_raw = keep.tile([P, PACK, M], F32, name="w8_raw", align_bytes=64)
-        w8_grouped = keep.tile([P, M, PACK], BF16, name="w8_grouped", align_bytes=64)
-        w8_codes = keep.tile([P, M], U32, name="w8_codes", align_bytes=64)
-        w8_plane = keep.tile([P, M], U8, name="w8_plane", align_bytes=64)
-        w4_codes = keep.tile([P, 2 * M], U8, name="w4_codes", align_bytes=64)
-        w4_plane = keep.tile([P, M // WORD], I32, name="w4_plane", align_bytes=64)
-        got_scales = keep.tile([P, S], U8, name="got_scales", align_bytes=64)
-        plane0 = keep.tile([P, S // WORD], I32, name="plane0", align_bytes=64)
-        got_words = [keep.tile([P, S], U32, name=f"got_words{a}", align_bytes=64) for a in range(2)]
+        tab_scales = keep.tile([P, T // WORD], I32, name="tab_scales", align_bytes=LINE)
+        tab_words = [keep.tile([P, T], I32, name=f"tab_words{a}", align_bytes=LINE) for a in range(2)]
+        w8_raw = keep.tile([P, PACK, M], F32, name="w8_raw", align_bytes=LINE)
+        w8_grouped = keep.tile([P, M, PACK], BF16, name="w8_grouped", align_bytes=LINE)
+        w8_codes = keep.tile([P, M], U32, name="w8_codes", align_bytes=LINE)
+        w8_plane = keep.tile([P, M], U8, name="w8_plane", align_bytes=LINE)
+        w4_codes = keep.tile([P, 2 * M], U8, name="w4_codes", align_bytes=LINE)
+        w4_plane = keep.tile([P, M // WORD], I32, name="w4_plane", align_bytes=LINE)
+        got_scales = keep.tile([P, S], U8, name="got_scales", align_bytes=LINE)
+        plane0 = keep.tile([P, S // WORD], I32, name="plane0", align_bytes=LINE)
+        got_words = [keep.tile([P, S], U32, name=f"got_words{a}", align_bytes=LINE) for a in range(2)]
 
         def plane_row(tile, r):
             return tile[r::QUAD, :]
@@ -128,7 +129,7 @@ def tile_list_tabo_none_kernel(tc, tab, w8, w4_words, w4_scales, offs, out):
         plane0_bytes = plane0[:].bitcast(U8)
         for s in range(SLICES):
             gather_words(0, s * N_SLICE, (s + 1) * N_SLICE)
-        results = [keep.tile([P, S], F32, name=f"result{h}") for h in range(HALVES)]
+        results = [keep.tile([P, S], F32, name=f"result{h}", align_bytes=LINE) for h in range(HALVES)]
         for s in range(SLICES):
             cols = slice(s * N_SLICE, (s + 1) * N_SLICE)
             order = (0, 1) if s == 1 else (1, 0)

from contextlib import ExitStack

import concourse.mybir as mybir

K_PASS, M, T, S = 512, 256, 1024, 512
FLOPS = 2 * 2 * K_PASS * M * S

F32 = mybir.dt.float32
BF16 = mybir.dt.bfloat16
I32 = mybir.dt.int32
U32 = mybir.dt.uint32
U16 = mybir.dt.uint16
U8 = mybir.dt.uint8
FP8X4 = mybir.dt.float8_e4m3fn_x4
FP4X4 = mybir.dt.float4_e2m1fn_x4

P = 128
PACK = 4
WORD = 4
GROUP = 16
QUADS = 4
QUAD = P // QUADS
ROWS = 4
PARKED = P - QUADS * ROWS
HALVES = M // P
N_SLICE = 128
SLICES = S // N_SLICE
PASS_LINES = P + QUADS
EARLY = 384
VECTOR_COLS = 96
LINE = 256
RUN = 4


def tile_list_tabo_none_kernel(tc, tab, w8, w4_words, w4_scales, offs, out):
    nc = tc.nc
    with ExitStack() as ctx:
        keep = ctx.enter_context(tc.tile_pool(name="keep", bufs=1))
        psum = ctx.enter_context(tc.psum_pool(name="psum", bufs=1))

        offsets = keep.tile([P, S // GROUP], U16, name="offsets")
        tab_scales = keep.tile([P, T // WORD], I32, name="tab_scales", align_bytes=LINE)
        tab_words = [keep.tile([P, T], I32, name=f"tab_words{a}", align_bytes=LINE) for a in range(2)]
        w8_raw = keep.tile([P, PACK, M], F32, name="w8_raw", align_bytes=LINE)
        w8_grouped = keep.tile([P, M, PACK], BF16, name="w8_grouped", align_bytes=LINE)
        w8_codes = keep.tile([P, M], U32, name="w8_codes", align_bytes=LINE)
        w8_plane = keep.tile([P, M], U8, name="w8_plane", align_bytes=LINE)
        w4_codes = keep.tile([P, 2 * M], U8, name="w4_codes", align_bytes=LINE)
        w4_plane = keep.tile([P, M // WORD], I32, name="w4_plane", align_bytes=LINE)
        got_scales = keep.tile([P, S], U8, name="got_scales", align_bytes=LINE)
        plane0 = keep.tile([P, S // WORD], I32, name="plane0", align_bytes=LINE)
        got_words = [keep.tile([P, S], U32, name=f"got_words{a}", align_bytes=LINE) for a in range(2)]

        def plane_row(tile, r):
            return tile[r::QUAD, :]

        scale_rows = tab[:, P * T * PACK :].rearrange("a (r t) -> a r t", t=T).bitcast(I32)
        nc.vector.memset(tab_scales[:PARKED, :], 0)
        nc.sync.dma_start(offsets[:], offs)
        nc.scalar.dma_start(tab_scales[PARKED:, :], scale_rows[0])

        w8_rows = w8.rearrange("(p j) m -> p (j m)", j=PACK)
        w8_flat = w8_raw[:].rearrange("p j m -> p (j m)")
        nc.sync.dma_start(w8_flat[:, :EARLY], w8_rows[:, :EARLY])

        for r in range(ROWS):
            queue = nc.scalar if r == 1 else nc.sync
            queue.dma_start(plane_row(tab_scales, r), scale_rows[1, r::ROWS])

        lines = tab.rearrange("a (g b) -> (a g) b", b=PACK * T).bitcast(I32)

        def load_words(a):
            nc.sync.dma_start(tab_words[a][:], lines[a * PASS_LINES : a * PASS_LINES + P, :])

        load_words(1)
        nc.vector.memset(w4_plane[:], 0)
        for r in range(ROWS):
            nc.sync.dma_start(plane_row(w4_plane, r), w4_scales[0].bitcast(I32)[r::ROWS])
            if r == 0:
                nc.sync.dma_start(w8_flat[:, EARLY:], w8_rows[:, EARLY:])
        nc.sync.dma_start(w4_codes[:].bitcast(I32), w4_words[0].bitcast(I32))
        load_words(0)
        nc.vector.memset(plane0[:], 0)

        nc.vector.tensor_copy(got_scales[:], tab_scales[:].bitcast(U8).indirect(offsets[:]))
        for r in range(ROWS):
            nc.sync.dma_start(plane_row(plane0, r), got_scales[:].bitcast(I32)[PARKED + r :: ROWS, :])

        def gather_words(a, lo, hi):
            nc.vector.tensor_copy(
                got_words[a][:, lo:hi],
                tab_words[a][:].bitcast(U32).indirect(offsets[:, lo // GROUP : hi // GROUP]),
            )

        banks = [[psum.tile([P, N_SLICE], F32, name=f"bank{s}_{h}") for h in range(HALVES)] for s in range(SLICES)]
        w4_bytes = w4_plane[:].bitcast(U8)
        for lo in range(0, S, S // 2):
            gather_words(1, lo, lo + S // 2)
        for s in range(SLICES):
            cols = slice(s * N_SLICE, (s + 1) * N_SLICE)
            for h in range(HALVES):
                nc.tensor.matmul_mx(
                    out=banks[s][h][:],
                    lhsT=w4_codes[:, 2 * P * h : 2 * P * (h + 1)].bitcast(FP4X4),
                    lhsT_scale=w4_bytes[:, P * h : P * (h + 1)],
                    rhs=got_words[1][:, cols].bitcast(FP8X4),
                    rhs_scale=got_scales[:, cols],
                    start=True,
                    stop=False,
                )

        for copy, ch in (
            (nc.scalar.copy, slice(P, M)),
            (nc.vector.tensor_copy, slice(0, VECTOR_COLS)),
            (nc.scalar.copy, slice(VECTOR_COLS, P)),
        ):
            copy(
                w8_grouped[:, ch, :].rearrange("p (c i) t -> p c t i", i=RUN),
                w8_raw[:, :, ch].rearrange("p t (c i) -> p c t i", i=RUN),
            )
        for h in reversed(range(HALVES)):
            ch = slice(P * h, P * (h + 1))
            nc.vector.quantize_mx(
                out=w8_codes[:, ch].bitcast(FP8X4),
                scales=w8_plane[:, ch],
                in_=w8_grouped[:, ch, :].rearrange("p m t -> p (m t)"),
            )

        plane0_bytes = plane0[:].bitcast(U8)
        for s in range(SLICES):
            gather_words(0, s * N_SLICE, (s + 1) * N_SLICE)
        results = [keep.tile([P, S], F32, name=f"result{h}", align_bytes=LINE) for h in range(HALVES)]
        for s in range(SLICES):
            cols = slice(s * N_SLICE, (s + 1) * N_SLICE)
            order = (0, 1) if s == 1 else (1, 0)
            for h in order:
                ch = slice(P * h, P * (h + 1))
                nc.tensor.matmul_mx(
                    out=banks[s][h][:],
                    lhsT=w8_codes[:, ch].bitcast(FP8X4),
                    lhsT_scale=w8_plane[:, ch],
                    rhs=got_words[0][:, cols].bitcast(FP8X4),
                    rhs_scale=plane0_bytes[:, cols],
                    start=False,
                    stop=True,
                )
            for h in order:
                is_last_bank = s == SLICES - 1 and h == order[-1]
                copy = nc.vector.tensor_copy if is_last_bank else nc.scalar.copy
                copy(results[h][:, cols], banks[s][h][:])
                if (s + h) % 2 or s == SLICES - 1:
                    first = s if h and s in (0, SLICES - 1) else s - 1
                    span = slice(first * N_SLICE, (s + 1) * N_SLICE)
                    nc.sync.dma_start(out[P * h : P * (h + 1), span], results[h][:, span])
